import numpy as np
import ml_dtypes


def mxq(x, axis, fmt="e4m3"):
    dtype, down = {"e4m3": (ml_dtypes.float8_e4m3fn, 7), "e5m2": (ml_dtypes.float8_e5m2, 14)}[fmt]
    v = np.moveaxis(np.asarray(x, np.float32).astype(ml_dtypes.bfloat16).astype(np.float64), axis, -1)
    blocks = v.reshape(v.shape[:-1] + (-1, 32))
    amax = np.abs(blocks).max(-1, keepdims=True)
    byte = np.maximum(np.where(amax > 0, np.frexp(amax)[1] - 1 + 127, 0) - down, 1)
    scale = np.exp2(byte - 127.0)
    codes = (blocks / scale).astype(np.float32).astype(dtype).astype(np.float64)
    return np.moveaxis((codes * scale).reshape(v.shape), -1, axis)


WIDE = False


def mx_kscale(k):
    if not WIDE:
        return np.ones(k)
    levels = np.array([10, -10, 5, -5, 0])
    if k % 512:
        return np.exp2(np.random.permutation(np.resize(levels, k // 32))).repeat(32)
    a = np.empty((k // 512, 16))
    for p in range(k // 512):
        a[p, :8] = np.random.permutation(np.resize(levels, 8))
        for g in range(8):
            far = levels[np.abs(levels - a[p, g]) >= 10]
            a[p, g + 8] = far[np.random.randint(len(far))]
    return np.exp2(a.ravel()).repeat(32)


def f64(x):
    return np.asarray(x).astype(np.float64)


def striped(idx):
    return np.tile(idx.reshape(-1, 16).T, (8, 1)).astype(np.uint16)


def unstriped(offs):
    return offs[:16].T.reshape(-1).astype(np.int64)


E2M1 = np.array([0.0, 0.5, 1.0, 1.5, 2.0, 3.0, 4.0, 6.0, -0.0, -0.5, -1.0, -1.5, -2.0, -3.0, -4.0, -6.0])


def pack_weight(w, fmt):
    k, n = w.shape
    w = f64(np.asarray(w, np.float32).astype(ml_dtypes.bfloat16)).reshape(k // 32, 32, n)
    amax = np.abs(w).max(1)
    if fmt == "e4m3":
        byte = np.frexp(amax)[1] - 1 + 127 - 7
    else:
        mant, ex = np.frexp(amax / 6.0)
        byte = np.where(mant > 0.5, ex, ex - 1) + 127
    byte = np.clip(np.where(amax > 0, byte, 1), 1, 254)
    scaled = (w * np.exp2(127.0 - byte)[:, None, :]).reshape(k, n).astype(np.float32)
    by_word = np.ascontiguousarray(scaled.reshape(k // 512, 128, 4, n).transpose(0, 1, 3, 2))
    if fmt == "e4m3":
        words = by_word.astype(ml_dtypes.float8_e4m3fn).view(np.uint8)
    else:
        c = by_word.astype(ml_dtypes.float4_e2m1fn).view(np.uint8) & 0xF
        words = (c[..., 0::2] | (c[..., 1::2] << 4)).reshape(k // 512, 128, 2 * n)
    return np.ascontiguousarray(words), np.ascontiguousarray(byte.astype(np.uint8).reshape(k // 512, 16, n))


def unpack_weight(words, scales, fmt):
    g, _, n = scales.shape
    words = np.ascontiguousarray(words).reshape(g, 128, n, -1)
    if fmt == "e4m3":
        vals = words.view(ml_dtypes.float8_e4m3fn).astype(np.float64)
    else:
        nib = np.empty((g, 128, n, 4), np.uint8)
        nib[..., 0::2] = words & 0xF
        nib[..., 1::2] = words >> 4
        vals = E2M1[nib]
    vals = vals * np.repeat(np.exp2(scales.astype(np.float64) - 127.0), 8, axis=1)[..., None]
    return vals.transpose(0, 1, 3, 2).reshape(g * 512, n)


def pack_table4(v):
    words, scales = pack_weight(v, "e2m1")
    g, t = words.shape[0] // 2, v.shape[1]
    words = words.reshape(g, 2, 128, t, 2).transpose(0, 2, 3, 1, 4)
    return np.concatenate([words.reshape(g, -1), scales.reshape(g, -1)], axis=1)


def unpack_table4(tab):
    g, t = tab.shape[0], tab.shape[1] // 544
    words = tab[:, :512 * t].reshape(g, 128, t, 2, 2).transpose(0, 3, 1, 2, 4).reshape(2 * g, 128, 2 * t)
    return unpack_weight(words, tab[:, 512 * t:].reshape(2 * g, 16, t), "e2m1")


K, M, T, S = 2048, 512, 4096, 1536


def setup_inputs():
    n = np.random.standard_normal
    s = mx_kscale(K)[:, None]
    return {
        "tab": pack_table4(n((K, T)) * s),
        "w": (n((K, M)) / np.sqrt(K) / s).astype(np.float32),
        "r": (n((512, 1536))).astype(np.float32),
        "offs": striped(np.random.permutation(T)[:S]),
    }


def reference(tab, w, r, offs):
    tab_ = unpack_table4(tab)[:, unstriped(offs)]
    w_ = mxq(f64(w), 0, "e4m3")
    y = w_.T @ tab_
    return f64(r) + y

@@ -1,0 +1,162 @@
+from contextlib import ExitStack
+
+import concourse.mybir as mybir
+
+K, M, T, S = 2048, 512, 4096, 1536
+FLOPS = 2 * K * M * S
+
+F32 = mybir.dt.float32
+BF16 = mybir.dt.bfloat16
+I32 = mybir.dt.int32
+U32 = mybir.dt.uint32
+U16 = mybir.dt.uint16
+U8 = mybir.dt.uint8
+E4M3X4 = mybir.dt.float8_e4m3fn_x4
+E2M1X4 = mybir.dt.float4_e2m1fn_x4
+ADD = mybir.AluOpType.add
+
+P = 128
+N = 512
+PASSES = 4
+PAIRS = 2
+NT = S // N
+MT = M // P
+
+
+def tile_list_tab4_res_kernel(tc, tab, w, r, offs, out):
+    nc = tc.nc
+    with ExitStack() as ctx:
+        keep = ctx.enter_context(tc.tile_pool(name="keep", bufs=1))
+        rows = ctx.enter_context(tc.tile_pool(name="rows", bufs=4))
+        psum = ctx.enter_context(tc.psum_pool(name="psum", bufs=8))
+
+        offsets = keep.tile([P, S // 16], U16, name="offsets")
+        scale_rows = keep.tile([P, T], U8, name="scale_rows", align_bytes=64)
+        picked_rows = keep.tile([P, S], U8, name="picked_rows", align_bytes=64)
+        table = [keep.tile([P, T], I32, name=f"table{m}", align_bytes=64) for m in range(PAIRS)]
+        picked = [keep.tile([P, S], U32, name=f"picked{m}", align_bytes=64) for m in range(PAIRS)]
+        codes = [keep.tile([P, 4 * S], U8, name=f"codes{m}", align_bytes=64) for m in range(PAIRS)]
+        scales = [keep.tile([P, S], U8, name=f"scales{a}", align_bytes=64) for a in range(PASSES)]
+        w_raw = [rows.tile([P, 4, M], F32, name=f"w_raw{a}", tag="rows", align_bytes=64) for a in range(PASSES)]
+        w_bf = [keep.tile([P, M, 4], BF16, name=f"w_bf{a}", align_bytes=64) for a in range(PASSES)]
+        w_codes = [keep.tile([P, M], U32, name=f"w_codes{a}", align_bytes=64) for a in range(PASSES)]
+        w_scales = [keep.tile([P, M], U8, name=f"w_scales{a}", align_bytes=64) for a in range(PASSES)]
+
+        nc.gpsimd.memset(scale_rows[64:128, :].bitcast(I32), 0)
+        for a in range(PASSES):
+            nc.gpsimd.memset(scales[a][:].bitcast(I32), 0)
+
+        nc.sync.dma_start(out=offsets[:], in_=offs)
+        for m in range(PAIRS):
+            nc.sync.dma_start(
+                out=scale_rows[32 * m : 32 * m + 32, :].bitcast(I32),
+                in_=tab[m : m + 1, 512 * T : 544 * T].rearrange("o (q t) -> (o q) t", t=T).bitcast(I32),
+            )
+
+        def load_table(m):
+            nc.sync.dma_start(
+                out=table[m][:],
+                in_=tab[m : m + 1, 0 : 512 * T].rearrange("o (p x) -> (o p) x", p=P).bitcast(I32),
+            )
+
+        def load_w(a):
+            nc.sync.dma_start(out=w_raw[a][:], in_=w[512 * a : 512 * (a + 1), :].rearrange("(p j) n -> p j n", j=4))
+
+        load_table(0)
+        load_w(0)
+        load_w(1)
+        load_table(1)
+        load_w(2)
+        load_w(3)
+
+        nc.vector.tensor_copy(picked_rows[:], scale_rows[:].indirect(offsets[:]))
+        for a in range(PASSES):
+            for q in range(4):
+                src = 16 * a + 4 * q
+                nc.gpsimd.dma_start(
+                    out=scales[a][32 * q : 32 * q + 4, :].bitcast(I32),
+                    in_=picked_rows[src : src + 4, :].bitcast(I32),
+                )
+
+        def gather(m, n):
+            nc.vector.tensor_copy(
+                picked[m][:, n * N : (n + 1) * N],
+                table[m][:].bitcast(U32).indirect(offsets[:, n * N // 16 : (n + 1) * N // 16]),
+            )
+
+        def part(m, n):
+            dst = codes[m][:].bitcast(U16).rearrange("p (h t) -> p h t", h=2)[:, :, n * N : (n + 1) * N]
+            src = picked[m][:, n * N : (n + 1) * N].bitcast(U16).rearrange("p (t h) -> p h t", h=2)
+            nc.vector.tensor_copy(dst, src)
+
+        def round_w(a):
+            nc.scalar.copy(w_bf[a][:], w_raw[a][:].rearrange("p j n -> p n j"))
+
+        def quantize_w(a):
+            nc.vector.quantize_mx(
+                out=w_codes[a][:].bitcast(E4M3X4),
+                scales=w_scales[a][:],
+                in_=w_bf[a][:].rearrange("p n j -> p (n j)"),
+            )
+
+        def gather_pair(m):
+            gather(m, 0)
+            gather(m, 1)
+            part(m, 0)
+            gather(m, 2)
+            part(m, 1)
+            part(m, 2)
+
+        def multiply(bank, a, n, t):
+            base = 2 * S * (a % 2) + 2 * N * n
+            nc.tensor.matmul_mx(
+                out=bank[:],
+                lhsT=w_codes[a][:, t * P : (t + 1) * P].bitcast(E4M3X4),
+                lhsT_scale=w_scales[a][:, t * P : (t + 1) * P],
+                rhs=codes[a // 2][:, base : base + 2 * N].bitcast(E2M1X4),
+                rhs_scale=scales[a][:, n * N : (n + 1) * N],
+                start=(a == 0),
+                stop=(a == PASSES - 1),
+            )
+
+        def finish(bank, n, t):
+            nc.vector.tensor_tensor(out=res[n][:, t, :], in0=bank[:], in1=res[n][:, t, :], op=ADD)
+            nc.sync.dma_start(out=out[t * P : (t + 1) * P, n * N : (n + 1) * N], in_=res[n][:, t, :])
+
+        res = []
+
+        def load_r(n):
+            tile_r = rows.tile([P, MT, N], F32, name=f"res{n}", tag="rows", align_bytes=64)
+            nc.sync.dma_start(out=tile_r[:], in_=r[:, n * N : (n + 1) * N].rearrange("(t p) j -> p t j", p=P))
+            res.append(tile_r)
+
+        gather_pair(0)
+        round_w(0)
+        quantize_w(0)
+        round_w(1)
+        quantize_w(1)
+        early = [(n, t) for n in range(2) for t in range(MT)]
+        banks = {}
+        for n, t in early:
+            bank = psum.tile([P, N], F32, name="bank")
+            banks[(n, t)] = bank
+        for a in (0, 1):
+            for n, t in early:
+                multiply(banks[(n, t)], a, n, t)
+        gather_pair(1)
+        round_w(2)
+        quantize_w(2)
+        for n, t in early:
+            multiply(banks[(n, t)], 2, n, t)
+        round_w(3)
+        quantize_w(3)
+        for n in range(NT):
+            load_r(n)
+        for n, t in early:
+            multiply(banks[(n, t)], 3, n, t)
+            finish(banks[(n, t)], n, t)
+        for t in range(MT):
+            bank = psum.tile([P, N], F32, name="bank")
+            for a in range(PASSES):
+                multiply(bank, a, 2, t)
+            finish(bank, 2, t)

@@ -36,22 +36,24 @@ def tile_list_tab4_res_kernel(tc, tab, w, r, offs, out):
         table = [keep.tile([P, T], I32, name=f"table{m}", align_bytes=64) for m in range(PAIRS)]
         picked = [keep.tile([P, S], U32, name=f"picked{m}", align_bytes=64) for m in range(PAIRS)]
         codes = [keep.tile([P, 4 * S], U8, name=f"codes{m}", align_bytes=64) for m in range(PAIRS)]
-        scales = [keep.tile([P, S], U8, name=f"scales{a}", align_bytes=64) for a in range(PASSES)]
+        scales = [picked_rows] + [keep.tile([P, S], U8, name=f"scales{a}", align_bytes=64) for a in range(1, PASSES)]
         w_raw = [rows.tile([P, 4, M], F32, name=f"w_raw{a}", tag="rows", align_bytes=64) for a in range(PASSES)]
         w_bf = [keep.tile([P, M, 4], BF16, name=f"w_bf{a}", align_bytes=64) for a in range(PASSES)]
         w_codes = [keep.tile([P, M], U32, name=f"w_codes{a}", align_bytes=64) for a in range(PASSES)]
         w_scales = [keep.tile([P, M], U8, name=f"w_scales{a}", align_bytes=64) for a in range(PASSES)]
 
-        nc.gpsimd.memset(scale_rows[64:128, :].bitcast(I32), 0)
-        for a in range(PASSES):
-            nc.gpsimd.memset(scales[a][:].bitcast(I32), 0)
+        nc.vector.memset(scale_rows[:].bitcast(I32), 0)
+        for a in range(1, PASSES):
+            nc.vector.memset(scales[a][96:128, :].bitcast(I32), 0)
 
         nc.sync.dma_start(out=offsets[:], in_=offs)
         for m in range(PAIRS):
-            nc.sync.dma_start(
-                out=scale_rows[32 * m : 32 * m + 32, :].bitcast(I32),
-                in_=tab[m : m + 1, 512 * T : 544 * T].rearrange("o (q t) -> (o q) t", t=T).bitcast(I32),
-            )
+            by_block = tab[m : m + 1, 512 * T : 544 * T].rearrange("o (h q t) -> (o h) q t", h=2, q=16)
+            for q in range(4):
+                nc.gpsimd.dma_start(
+                    out=scale_rows[32 * q + 8 * m : 32 * q + 8 * m + 8, :].bitcast(I32),
+                    in_=by_block[:, 4 * q : 4 * q + 4, :].bitcast(I32),
+                )
 
         def load_table(m):
             nc.sync.dma_start(
@@ -70,13 +72,11 @@ def tile_list_tab4_res_kernel(tc, tab, w, r, offs, out):
         load_w(3)
 
         nc.vector.tensor_copy(picked_rows[:], scale_rows[:].indirect(offsets[:]))
-        for a in range(PASSES):
-            for q in range(4):
-                src = 16 * a + 4 * q
-                nc.gpsimd.dma_start(
-                    out=scales[a][32 * q : 32 * q + 4, :].bitcast(I32),
-                    in_=picked_rows[src : src + 4, :].bitcast(I32),
-                )
+        for a in range(1, PASSES):
+            nc.gpsimd.dma_start(
+                out=scales[a][0:112, :].bitcast(I32),
+                in_=picked_rows[4 * a : 4 * a + 112, :].bitcast(I32),
+            )
 
         def gather(m, n):
             nc.vector.tensor_copy(
@@ -90,7 +90,12 @@ def tile_list_tab4_res_kernel(tc, tab, w, r, offs, out):
             nc.vector.tensor_copy(dst, src)
 
         def round_w(a):
-            nc.scalar.copy(w_bf[a][:], w_raw[a][:].rearrange("p j n -> p n j"))
+            if a < PASSES - 1:
+                nc.scalar.copy(w_bf[a][:], w_raw[a][:].rearrange("p j n -> p n j"))
+            else:
+                half = M // 2
+                nc.scalar.copy(w_bf[a][:, 0:half, :], w_raw[a][:, :, 0:half].rearrange("p j n -> p n j"))
+                nc.vector.tensor_copy(w_bf[a][:, half:M, :], w_raw[a][:, :, half:M].rearrange("p j n -> p n j"))
 
         def quantize_w(a):
             nc.vector.quantize_mx(

@@ -27,61 +27,80 @@ def tile_list_tab4_res_kernel(tc, tab, w, r, offs, out):
     nc = tc.nc
     with ExitStack() as ctx:
         keep = ctx.enter_context(tc.tile_pool(name="keep", bufs=1))
-        rows = ctx.enter_context(tc.tile_pool(name="rows", bufs=4))
+        late_pool = ctx.enter_context(tc.tile_pool(name="late_pool", bufs=1))
         psum = ctx.enter_context(tc.psum_pool(name="psum", bufs=8))
 
         offsets = keep.tile([P, S // 16], U16, name="offsets")
-        scale_rows = keep.tile([P, T], U8, name="scale_rows", align_bytes=64)
+        scale_rows = late_pool.tile([P, T], U8, name="scale_rows", offset=4 * T - T // 2)
         picked_rows = keep.tile([P, S], U8, name="picked_rows", align_bytes=64)
-        table = [keep.tile([P, T], I32, name=f"table{m}", align_bytes=64) for m in range(PAIRS)]
+        table0 = keep.tile([P, T], I32, name="table0", align_bytes=64)
+        w_first = [keep.tile([P, 4, M], F32, name=f"w_first{a}", align_bytes=64) for a in range(2)]
         picked = [keep.tile([P, S], U32, name=f"picked{m}", align_bytes=64) for m in range(PAIRS)]
         codes = [keep.tile([P, 4 * S], U8, name=f"codes{m}", align_bytes=64) for m in range(PAIRS)]
-        scales = [picked_rows] + [keep.tile([P, S], U8, name=f"scales{a}", align_bytes=64) for a in range(1, PASSES)]
-        w_raw = [rows.tile([P, 4, M], F32, name=f"w_raw{a}", tag="rows", align_bytes=64) for a in range(PASSES)]
+        scales = [keep.tile([P, S], U8, name=f"scales{a}", align_bytes=64) for a in range(PASSES)]
         w_bf = [keep.tile([P, M, 4], BF16, name=f"w_bf{a}", align_bytes=64) for a in range(PASSES)]
         w_codes = [keep.tile([P, M], U32, name=f"w_codes{a}", align_bytes=64) for a in range(PASSES)]
         w_scales = [keep.tile([P, M], U8, name=f"w_scales{a}", align_bytes=64) for a in range(PASSES)]
 
-        nc.vector.memset(scale_rows[:].bitcast(I32), 0)
-        for a in range(1, PASSES):
-            nc.vector.memset(scales[a][96:128, :].bitcast(I32), 0)
-
+        nc.gpsimd.memset(scale_rows[64:128, :].bitcast(I32), 0)
+        for a in range(PASSES):
+            nc.gpsimd.memset(scales[a][:].bitcast(I32), 0)
         nc.sync.dma_start(out=offsets[:], in_=offs)
         for m in range(PAIRS):
-            by_block = tab[m : m + 1, 512 * T : 544 * T].rearrange("o (h q t) -> (o h) q t", h=2, q=16)
-            for q in range(4):
-                nc.gpsimd.dma_start(
-                    out=scale_rows[32 * q + 8 * m : 32 * q + 8 * m + 8, :].bitcast(I32),
-                    in_=by_block[:, 4 * q : 4 * q + 4, :].bitcast(I32),
-                )
+            nc.sync.dma_start(
+                out=scale_rows[32 * m : 32 * m + 32, :].bitcast(I32),
+                in_=tab[m : m + 1, 512 * T : 544 * T].rearrange("o (q t) -> (o q) t", t=T).bitcast(I32),
+            )
 
         def load_table(m):
             nc.sync.dma_start(
-                out=table[m][:],
-                in_=tab[m : m + 1, 0 : 512 * T].rearrange("o (p x) -> (o p) x", p=P).bitcast(I32),
+                out=table[m], in_=tab[m : m + 1, 0 : 512 * T].rearrange("o (p x) -> (o p) x", p=P).bitcast(I32)
             )
 
         def load_w(a):
-            nc.sync.dma_start(out=w_raw[a][:], in_=w[512 * a : 512 * (a + 1), :].rearrange("(p j) n -> p j n", j=4))
+            nc.sync.dma_start(out=w_raw[a], in_=w[512 * a : 512 * (a + 1), :].rearrange("(p j) n -> p j n", j=4))
 
+        def load_r(view, first, width):
+            nc.sync.dma_start(out=view, in_=r[:, first : first + width].rearrange("(t p) j -> p t j", p=P))
+
+        def move(a):
+            for q in range(4):
+                nc.sync.dma_start(
+                    out=scales[a][32 * q : 32 * q + 4, :].bitcast(I32),
+                    in_=picked_rows[16 * a + 4 * q : 16 * a + 4 * q + 4, :].bitcast(I32),
+                )
+
+        table = [table0[:]]
+        w_raw = [t[:] for t in w_first]
         load_table(0)
         load_w(0)
         load_w(1)
-        load_table(1)
-        load_w(2)
-        load_w(3)
 
         nc.vector.tensor_copy(picked_rows[:], scale_rows[:].indirect(offsets[:]))
-        for a in range(1, PASSES):
-            nc.gpsimd.dma_start(
-                out=scales[a][0:112, :].bitcast(I32),
-                in_=picked_rows[4 * a : 4 * a + 112, :].bitcast(I32),
-            )
+        table1 = late_pool.tile([P, T], I32, name="table1", offset=0)
+        late = late_pool.tile([P, 4 * 2 * M + MT * S], F32, name="late", offset=4 * T)
+        table.append(table1[:])
+        for i in range(2):
+            w_raw.append(late[:, 4 * M * i : 4 * M * (i + 1)].rearrange("p (j n) -> p j n", j=4))
+        r_first = 4 * 2 * M
+        r01 = late[:, r_first : r_first + MT * 2 * N].rearrange("p (t j) -> p t j", t=MT)
+        r2 = late[:, r_first + MT * 2 * N : r_first + MT * S].rearrange("p (t j) -> p t j", t=MT)
+        res = [r01[:, :, 0:N], r01[:, :, N : 2 * N], r2]
+
+        move(0)
+        load_table(1)
+        move(1)
+        load_w(2)
+        move(2)
+        load_w(3)
+        move(3)
+        load_r(r01, 0, 2 * N)
+        load_r(r2, 2 * N, N)
 
         def gather(m, n):
             nc.vector.tensor_copy(
                 picked[m][:, n * N : (n + 1) * N],
-                table[m][:].bitcast(U32).indirect(offsets[:, n * N // 16 : (n + 1) * N // 16]),
+                table[m].bitcast(U32).indirect(offsets[:, n * N // 16 : (n + 1) * N // 16]),
             )
 
         def part(m, n):
@@ -91,7 +110,7 @@ def tile_list_tab4_res_kernel(tc, tab, w, r, offs, out):
 
         def round_w(a):
             if a < PASSES - 1:
-                nc.scalar.copy(w_bf[a][:], w_raw[a][:].rearrange("p j n -> p n j"))
+                nc.scalar.copy(w_bf[a][:], w_raw[a].rearrange("p j n -> p n j"))
             else:
                 half = M // 2
                 nc.scalar.copy(w_bf[a][:, 0:half, :], w_raw[a][:, :, 0:half].rearrange("p j n -> p n j"))
@@ -128,13 +147,6 @@ def tile_list_tab4_res_kernel(tc, tab, w, r, offs, out):
             nc.vector.tensor_tensor(out=res[n][:, t, :], in0=bank[:], in1=res[n][:, t, :], op=ADD)
             nc.sync.dma_start(out=out[t * P : (t + 1) * P, n * N : (n + 1) * N], in_=res[n][:, t, :])
 
-        res = []
-
-        def load_r(n):
-            tile_r = rows.tile([P, MT, N], F32, name=f"res{n}", tag="rows", align_bytes=64)
-            nc.sync.dma_start(out=tile_r[:], in_=r[:, n * N : (n + 1) * N].rearrange("(t p) j -> p t j", p=P))
-            res.append(tile_r)
-
         gather_pair(0)
         round_w(0)
         quantize_w(0)
@@ -155,8 +167,6 @@ def tile_list_tab4_res_kernel(tc, tab, w, r, offs, out):
             multiply(banks[(n, t)], 2, n, t)
         round_w(3)
         quantize_w(3)
-        for n in range(NT):
-            load_r(n)
         for n, t in early:
             multiply(banks[(n, t)], 3, n, t)
             finish(banks[(n, t)], n, t)

from contextlib import ExitStack

import concourse.mybir as mybir

K, M, T, S = 2048, 512, 4096, 1536
FLOPS = 2 * K * M * S

F32 = mybir.dt.float32
BF16 = mybir.dt.bfloat16
I32 = mybir.dt.int32
U32 = mybir.dt.uint32
U16 = mybir.dt.uint16
U8 = mybir.dt.uint8
E4M3X4 = mybir.dt.float8_e4m3fn_x4
E2M1X4 = mybir.dt.float4_e2m1fn_x4
ADD = mybir.AluOpType.add

P = 128
N = 512
PASSES = 4
PAIRS = 2
NT = S // N
MT = M // P


def tile_list_tab4_res_kernel(tc, tab, w, r, offs, out):
    nc = tc.nc
    with ExitStack() as ctx:
        keep = ctx.enter_context(tc.tile_pool(name="keep", bufs=1))
        late_pool = ctx.enter_context(tc.tile_pool(name="late_pool", bufs=1))
        psum = ctx.enter_context(tc.psum_pool(name="psum", bufs=8))

        offsets = keep.tile([P, S // 16], U16, name="offsets")
        scale_rows = late_pool.tile([P, T], U8, name="scale_rows", offset=4 * T - T // 2)
        picked_rows = keep.tile([P, S], U8, name="picked_rows", align_bytes=64)
        table0 = keep.tile([P, T], I32, name="table0", align_bytes=64)
        w_first = [keep.tile([P, 4, M], F32, name=f"w_first{a}", align_bytes=64) for a in range(2)]
        picked = [keep.tile([P, S], U32, name=f"picked{m}", align_bytes=64) for m in range(PAIRS)]
        codes = [keep.tile([P, 4 * S], U8, name=f"codes{m}", align_bytes=64) for m in range(PAIRS)]
        scales = [keep.tile([P, S], U8, name=f"scales{a}", align_bytes=64) for a in range(PASSES)]
        w_bf = [keep.tile([P, M, 4], BF16, name=f"w_bf{a}", align_bytes=64) for a in range(PASSES)]
        w_codes = [keep.tile([P, M], U32, name=f"w_codes{a}", align_bytes=64) for a in range(PASSES)]
        w_scales = [keep.tile([P, M], U8, name=f"w_scales{a}", align_bytes=64) for a in range(PASSES)]

        nc.gpsimd.memset(scale_rows[64:128, :].bitcast(I32), 0)
        for a in range(PASSES):
            nc.gpsimd.memset(scales[a][:].bitcast(I32), 0)
        nc.sync.dma_start(out=offsets[:], in_=offs)
        for m in range(PAIRS):
            nc.sync.dma_start(
                out=scale_rows[32 * m : 32 * m + 32, :].bitcast(I32),
                in_=tab[m : m + 1, 512 * T : 544 * T].rearrange("o (q t) -> (o q) t", t=T).bitcast(I32),
            )

        def load_table(m):
            nc.sync.dma_start(
                out=table[m], in_=tab[m : m + 1, 0 : 512 * T].rearrange("o (p x) -> (o p) x", p=P).bitcast(I32)
            )

        def load_w(a):
            nc.sync.dma_start(out=w_raw[a], in_=w[512 * a : 512 * (a + 1), :].rearrange("(p j) n -> p j n", j=4))

        def load_r(view, first, width):
            nc.sync.dma_start(out=view, in_=r[:, first : first + width].rearrange("(t p) j -> p t j", p=P))

        def move(a):
            for q in range(4):
                nc.sync.dma_start(
                    out=scales[a][32 * q : 32 * q + 4, :].bitcast(I32),
                    in_=picked_rows[16 * a + 4 * q : 16 * a + 4 * q + 4, :].bitcast(I32),
                )

        table = [table0[:]]
        w_raw = [t[:] for t in w_first]
        load_table(0)
        load_w(0)
        load_w(1)

        nc.vector.tensor_copy(picked_rows[:], scale_rows[:].indirect(offsets[:]))
        table1 = late_pool.tile([P, T], I32, name="table1", offset=0)
        late = late_pool.tile([P, 4 * 2 * M + MT * S], F32, name="late", offset=4 * T)
        table.append(table1[:])
        for i in range(2):
            w_raw.append(late[:, 4 * M * i : 4 * M * (i + 1)].rearrange("p (j n) -> p j n", j=4))
        r_first = 4 * 2 * M
        r01 = late[:, r_first : r_first + MT * 2 * N].rearrange("p (t j) -> p t j", t=MT)
        r2 = late[:, r_first + MT * 2 * N : r_first + MT * S].rearrange("p (t j) -> p t j", t=MT)
        res = [r01[:, :, 0:N], r01[:, :, N : 2 * N], r2]

        move(0)
        load_table(1)
        move(1)
        load_w(2)
        move(2)
        load_w(3)
        move(3)
        load_r(r01, 0, 2 * N)
        load_r(r2, 2 * N, N)

        def gather(m, n):
            nc.vector.tensor_copy(
                picked[m][:, n * N : (n + 1) * N],
                table[m].bitcast(U32).indirect(offsets[:, n * N // 16 : (n + 1) * N // 16]),
            )

        def part(m, n):
            dst = codes[m][:].bitcast(U16).rearrange("p (h t) -> p h t", h=2)[:, :, n * N : (n + 1) * N]
            src = picked[m][:, n * N : (n + 1) * N].bitcast(U16).rearrange("p (t h) -> p h t", h=2)
            nc.vector.tensor_copy(dst, src)

        def round_w(a):
            if a < PASSES - 1:
                nc.scalar.copy(w_bf[a][:], w_raw[a].rearrange("p j n -> p n j"))
            else:
                half = M // 2
                nc.scalar.copy(w_bf[a][:, 0:half, :], w_raw[a][:, :, 0:half].rearrange("p j n -> p n j"))
                nc.vector.tensor_copy(w_bf[a][:, half:M, :], w_raw[a][:, :, half:M].rearrange("p j n -> p n j"))

        def quantize_w(a):
            nc.vector.quantize_mx(
                out=w_codes[a][:].bitcast(E4M3X4),
                scales=w_scales[a][:],
                in_=w_bf[a][:].rearrange("p n j -> p (n j)"),
            )

        def gather_pair(m):
            gather(m, 0)
            gather(m, 1)
            part(m, 0)
            gather(m, 2)
            part(m, 1)
            part(m, 2)

        def multiply(bank, a, n, t):
            base = 2 * S * (a % 2) + 2 * N * n
            nc.tensor.matmul_mx(
                out=bank[:],
                lhsT=w_codes[a][:, t * P : (t + 1) * P].bitcast(E4M3X4),
                lhsT_scale=w_scales[a][:, t * P : (t + 1) * P],
                rhs=codes[a // 2][:, base : base + 2 * N].bitcast(E2M1X4),
                rhs_scale=scales[a][:, n * N : (n + 1) * N],
                start=(a == 0),
                stop=(a == PASSES - 1),
            )

        def finish(bank, n, t):
            nc.vector.tensor_tensor(out=res[n][:, t, :], in0=bank[:], in1=res[n][:, t, :], op=ADD)
            nc.sync.dma_start(out=out[t * P : (t + 1) * P, n * N : (n + 1) * N], in_=res[n][:, t, :])

        gather_pair(0)
        round_w(0)
        quantize_w(0)
        round_w(1)
        quantize_w(1)
        early = [(n, t) for n in range(2) for t in range(MT)]
        banks = {}
        for n, t in early:
            bank = psum.tile([P, N], F32, name="bank")
            banks[(n, t)] = bank
        for a in (0, 1):
            for n, t in early:
                multiply(banks[(n, t)], a, n, t)
        gather_pair(1)
        round_w(2)
        quantize_w(2)
        for n, t in early:
            multiply(banks[(n, t)], 2, n, t)
        round_w(3)
        quantize_w(3)
        for n, t in early:
            multiply(banks[(n, t)], 3, n, t)
            finish(banks[(n, t)], n, t)
        for t in range(MT):
            bank = psum.tile([P, N], F32, name="bank")
            for a in range(PASSES):
                multiply(bank, a, 2, t)
            finish(bank, 2, t)
